import numpy as np
import ml_dtypes


def mxq(x, axis, fmt="e4m3"):
    dtype, down = {"e4m3": (ml_dtypes.float8_e4m3fn, 7), "e5m2": (ml_dtypes.float8_e5m2, 14)}[fmt]
    v = np.moveaxis(np.asarray(x, np.float32).astype(ml_dtypes.bfloat16).astype(np.float64), axis, -1)
    blocks = v.reshape(v.shape[:-1] + (-1, 32))
    amax = np.abs(blocks).max(-1, keepdims=True)
    byte = np.maximum(np.where(amax > 0, np.frexp(amax)[1] - 1 + 127, 0) - down, 1)
    scale = np.exp2(byte - 127.0)
    codes = (blocks / scale).astype(np.float32).astype(dtype).astype(np.float64)
    return np.moveaxis((codes * scale).reshape(v.shape), -1, axis)


WIDE = False


def mx_kscale(k):
    if not WIDE:
        return np.ones(k)
    levels = np.array([10, -10, 5, -5, 0])
    if k % 512:
        return np.exp2(np.random.permutation(np.resize(levels, k // 32))).repeat(32)
    a = np.empty((k // 512, 16))
    for p in range(k // 512):
        a[p, :8] = np.random.permutation(np.resize(levels, 8))
        for g in range(8):
            far = levels[np.abs(levels - a[p, g]) >= 10]
            a[p, g + 8] = far[np.random.randint(len(far))]
    return np.exp2(a.ravel()).repeat(32)


def f64(x):
    return np.asarray(x).astype(np.float64)


def striped8(idx):
    return np.concatenate([v.reshape(-1, 16).T for v in idx]).astype(np.uint16)


def unstriped8(offs):
    return np.stack([offs[16 * g:16 * g + 16].T.reshape(-1) for g in range(8)]).astype(np.int64)


def gelu(v):
    return 0.5 * v * (1.0 + np.tanh(np.sqrt(2.0 / np.pi) * (v + 0.044715 * v**3)))


K, M, T, S = 1536, 1024, 512, 256


def setup_inputs():
    n = np.random.standard_normal
    s = mx_kscale(K)[:, None]
    return {
        "x": (n((K, S)) * s).astype(np.float32),
        "w": (n((K, M)) / np.sqrt(K) / s).astype(np.float32),
        "b": (0.3 * n(1024)).astype(np.float32),
        "wgo": np.repeat(np.random.uniform(0.5, 2.0, (8, S)), 16, axis=0).astype(np.float32),
        "offs": striped8(np.stack([np.random.permutation(T)[:S] for _ in range(8)])),
    }


def reference(x, w, b, wgo, offs):
    x_ = mxq(f64(x), 0, "e4m3")
    w_ = mxq(f64(w), 0, "e4m3")
    y = w_.T @ x_
    place = unstriped8(offs)[np.arange(M) % 128 // 16]
    out = np.zeros((M, T))
    out[np.arange(M)[:, None], place] = f64(wgo)[np.arange(M) % 128] * (gelu(y + f64(b)[:, None]))
    return out

@@ -1,0 +1,167 @@
+from contextlib import ExitStack
+
+import concourse.mybir as mybir
+from concourse.masks import make_identity
+
+K, M, T, S = 1536, 1024, 512, 256
+FLOPS = 2 * K * M * S
+
+F32 = mybir.dt.float32
+BF16 = mybir.dt.bfloat16
+U32 = mybir.dt.uint32
+U16 = mybir.dt.uint16
+U8 = mybir.dt.uint8
+FP8X4 = mybir.dt.float8_e4m3fn_x4
+GELU = mybir.ActivationFunctionType.Gelu_apprx_tanh
+MULT = mybir.AluOpType.mult
+
+P = 128
+PACK = 4
+K_PASS = P * PACK
+PASSES = K // K_PASS
+HALF = S // 2
+LIST_COLS = HALF // 16
+
+BLOCKS = [(0, 1), (1, 1), (2, 2), (4, 2), (6, 1), (7, 1)]
+
+
+def interleave(copy, grouped, raw):
+    copy(
+        out=grouped.rearrange("p (c i) t -> p c t i", i=4),
+        in_=raw.rearrange("p t (c i) -> p c t i", i=4),
+    )
+
+
+def tile_list_hscat_gelu_kernel(tc, x, w, b, wgo, offs, out):
+    nc = tc.nc
+    with ExitStack() as ctx:
+        keep = ctx.enter_context(tc.tile_pool(name="keep", bufs=1))
+        acc_pool = ctx.enter_context(tc.psum_pool(name="acc", bufs=7))
+        bias_pool = ctx.enter_context(tc.psum_pool(name="bias", bufs=1))
+
+        offsets = keep.tile([P, S // 16], U16, name="offsets")
+        weights = keep.tile([P, S], F32, name="weights")
+        bias_rows = keep.tile([P, P], F32, name="bias_rows")
+        bias = keep.tile([P, M // P], F32, name="bias_cols")
+        ident = keep.tile([P, P], F32, name="ident")
+        warm = keep.tile([P, 1], F32, name="warm")
+
+        x_codes = [keep.tile([P, S], U32, align_bytes=64, name=f"x_codes{a}") for a in range(PASSES)]
+        x_scales = [keep.tile([P, S], U8, align_bytes=64, name=f"x_scales{a}") for a in range(PASSES)]
+        windows = [keep.tile([P, T], F32, name=f"window{m}") for m in range(M // P)]
+        values = [keep.tile([P, S], F32, name=f"values{m}") for m in range(M // P)]
+
+        nc.vector.memset(warm[:], 0.0)
+        nc.scalar.activation(warm[:], warm[:], GELU)
+        nc.gpsimd.memset(bias_rows[:], 0.0)
+
+        def load(src, name):
+            width = src.shape[1]
+            raw = keep.tile([P, PACK, width], F32, name=f"{name}_raw")
+            nc.sync.dma_start(out=raw[:], in_=src.rearrange("(p j) n -> p j n", j=PACK))
+            return raw
+
+        def rows(a):
+            return slice(a * K_PASS, (a + 1) * K_PASS)
+
+        def cast(engine, raw, name):
+            width = raw.shape[2]
+            grouped = keep.tile([P, width, PACK], BF16, align_bytes=64, name=f"{name}_grouped")
+            copy = nc.vector.tensor_copy if engine == "V" else nc.scalar.copy
+            interleave(copy, grouped[:], raw[:])
+            return grouped
+
+        def quantize(grouped, codes, scales):
+            nc.vector.quantize_mx(out=codes.bitcast(FP8X4), scales=scales, in_=grouped[:].rearrange("p n j -> p (n j)"))
+
+        x_raw = {}
+        w_raw = {}
+        for a in range(PASSES):
+            x_raw[0, a] = load(x[rows(a), 0:HALF], f"x0_{a}")
+            w_raw[0, a] = load(w[rows(a), 0:P], f"w0_{a}")
+        nc.sync.dma_start(out=bias_rows[0 : M // P, :], in_=b.rearrange("(c p) -> c p", p=P))
+        nc.sync.dma_start(offsets[:], offs)
+        nc.sync.dma_start(out=weights[:], in_=wgo)
+        for a in range(PASSES):
+            x_raw[1, a] = load(x[rows(a), HALF:S], f"x1_{a}")
+        for i, (m0, count) in enumerate(BLOCKS):
+            if i > 0:
+                for a in range(PASSES):
+                    w_raw[i, a] = load(w[rows(a), m0 * P : (m0 + count) * P], f"w{i}_{a}")
+
+        for m in range(M // P):
+            nc.vector.memset(windows[m][:], 0.0)
+
+        make_identity(nc, ident[:])
+        bias_ps = bias_pool.tile([P, P], F32, name="bias_ps")
+        nc.tensor.transpose(bias_ps[:], bias_rows[:], ident[:])
+        nc.scalar.copy(out=bias[:], in_=bias_ps[:, 0 : M // P])
+
+        w_codes = {}
+        w_scales = {}
+
+        def w_cast(i, engines):
+            return [cast(engines[a], w_raw[i, a], f"w{i}_{a}") for a in range(PASSES)]
+
+        def w_quantize(i, a, grouped):
+            width = BLOCKS[i][1] * P
+            w_codes[i, a] = keep.tile([P, width], U32, align_bytes=64, name=f"w_codes{i}_{a}")
+            w_scales[i, a] = keep.tile([P, width], U8, align_bytes=64, name=f"w_scales{i}_{a}")
+            quantize(grouped, w_codes[i, a][:], w_scales[i, a][:])
+
+        def multiply(i, sub, s0, s1):
+            m = BLOCKS[i][0] + sub
+            cols = slice(sub * P, (sub + 1) * P)
+            acc = acc_pool.tile([P, S], F32, name="acc")
+            for a in range(PASSES):
+                nc.tensor.matmul_mx(
+                    out=acc[:, s0:s1],
+                    lhsT=w_codes[i, a][:, cols].bitcast(FP8X4),
+                    lhsT_scale=w_scales[i, a][:, cols],
+                    rhs=x_codes[a][:, s0:s1].bitcast(FP8X4),
+                    rhs_scale=x_scales[a][:, s0:s1],
+                    start=(a == 0),
+                    stop=(a == PASSES - 1),
+                )
+            nc.scalar.activation(values[m][:, s0:s1], acc[:, s0:s1], GELU, bias=bias[:, m : m + 1])
+
+        def scatter(m, h):
+            js = slice(h * HALF, (h + 1) * HALF)
+            nc.vector.tensor_tensor(
+                windows[m][:].indirect(offsets[:, h * LIST_COLS : (h + 1) * LIST_COLS]),
+                values[m][:, js],
+                weights[:, js],
+                MULT,
+            )
+
+        def store(m):
+            nc.sync.dma_start(out=out[m * P : (m + 1) * P, :], in_=windows[m][:])
+
+        for a in range(PASSES):
+            gx = cast("V", x_raw[0, a], f"x0_{a}")
+            gw = cast("S", w_raw[0, a], f"w0_{a}")
+            quantize(gx, x_codes[a][:, 0:HALF], x_scales[a][:, 0:HALF])
+            w_quantize(0, a, gw)
+        multiply(0, 0, 0, HALF)
+        gx1 = [cast("SSV"[a], x_raw[1, a], f"x1_{a}") for a in range(PASSES)]
+        scatter(0, 0)
+        for a in range(PASSES):
+            quantize(gx1[a], x_codes[a][:, HALF:S], x_scales[a][:, HALF:S])
+        multiply(0, 0, HALF, S)
+        pending = [(0, 1)]
+        for i in range(1, len(BLOCKS)):
+            grouped = w_cast(i, "SSS")
+            for a in range(PASSES):
+                w_quantize(i, a, grouped[a])
+            m0, count = BLOCKS[i]
+            for sub in range(count):
+                multiply(i, sub, 0, S)
+            for m, h in pending:
+                scatter(m, h)
+                if h == 1:
+                    store(m)
+            pending = [(m0 + sub, h) for h in range(2) for sub in range(count)]
+        for m, h in pending:
+            scatter(m, h)
+            if h == 1:
+                store(m)

@@ -21,15 +21,9 @@ K_PASS = P * PACK
 PASSES = K // K_PASS
 HALF = S // 2
 LIST_COLS = HALF // 16
+TILES = M // P
 
 BLOCKS = [(0, 1), (1, 1), (2, 2), (4, 2), (6, 1), (7, 1)]
-
-
-def interleave(copy, grouped, raw):
-    copy(
-        out=grouped.rearrange("p (c i) t -> p c t i", i=4),
-        in_=raw.rearrange("p t (c i) -> p c t i", i=4),
-    )
 
 
 def tile_list_hscat_gelu_kernel(tc, x, w, b, wgo, offs, out):
@@ -42,87 +36,64 @@ def tile_list_hscat_gelu_kernel(tc, x, w, b, wgo, offs, out):
         offsets = keep.tile([P, S // 16], U16, name="offsets")
         weights = keep.tile([P, S], F32, name="weights")
         bias_rows = keep.tile([P, P], F32, name="bias_rows")
-        bias = keep.tile([P, M // P], F32, name="bias_cols")
+        bias = keep.tile([P, TILES], F32, name="bias_cols")
         ident = keep.tile([P, P], F32, name="ident")
         warm = keep.tile([P, 1], F32, name="warm")
-
-        x_codes = [keep.tile([P, S], U32, align_bytes=64, name=f"x_codes{a}") for a in range(PASSES)]
-        x_scales = [keep.tile([P, S], U8, align_bytes=64, name=f"x_scales{a}") for a in range(PASSES)]
-        windows = [keep.tile([P, T], F32, name=f"window{m}") for m in range(M // P)]
-        values = [keep.tile([P, S], F32, name=f"values{m}") for m in range(M // P)]
+        windows = [keep.tile([P, T], F32, name=f"window{m}") for m in range(TILES)]
+        values = [keep.tile([P, S], F32, name=f"values{m}") for m in range(TILES)]
 
         nc.vector.memset(warm[:], 0.0)
         nc.scalar.activation(warm[:], warm[:], GELU)
         nc.gpsimd.memset(bias_rows[:], 0.0)
 
-        def load(src, name):
+        def operand(name, src):
             width = src.shape[1]
-            raw = keep.tile([P, PACK, width], F32, name=f"{name}_raw")
-            nc.sync.dma_start(out=raw[:], in_=src.rearrange("(p j) n -> p j n", j=PACK))
-            return raw
+            raw = keep.tile([P, PACK, PASSES, width], F32, name=f"{name}_raw")
+            grouped = keep.tile([P, PASSES * width, PACK], BF16, align_bytes=64, name=f"{name}_grouped")
+            codes = keep.tile([P, PASSES * width], U32, align_bytes=64, name=f"{name}_codes")
+            scales = keep.tile([P, PASSES * width], U8, align_bytes=64, name=f"{name}_scales")
+            return src, width, raw, grouped, codes, scales
 
-        def rows(a):
-            return slice(a * K_PASS, (a + 1) * K_PASS)
+        def load(op, a, engine=nc.sync):
+            src, width, raw, grouped, codes, scales = op
+            rows = src[a * K_PASS : (a + 1) * K_PASS, :]
+            engine.dma_start(out=raw[:, :, a, :], in_=rows.rearrange("(p j) n -> p j n", j=PACK))
 
-        def cast(engine, raw, name):
-            width = raw.shape[2]
-            grouped = keep.tile([P, width, PACK], BF16, align_bytes=64, name=f"{name}_grouped")
+        def cast(op, a0, a1, engine, c0=0, c1=None):
+            src, width, raw, grouped, codes, scales = op
             copy = nc.vector.tensor_copy if engine == "V" else nc.scalar.copy
-            interleave(copy, grouped[:], raw[:])
-            return grouped
+            lo, hi = a0 * width, a1 * width
+            copy(
+                out=grouped[:, lo:hi, :].rearrange("p (c i) t -> p c t i", i=4),
+                in_=raw[:].rearrange("p t a n -> p t (a n)")[:, :, lo:hi].rearrange("p t (c i) -> p c t i", i=4),
+            )
 
-        def quantize(grouped, codes, scales):
-            nc.vector.quantize_mx(out=codes.bitcast(FP8X4), scales=scales, in_=grouped[:].rearrange("p n j -> p (n j)"))
+        def quantize(op, a0, a1):
+            src, width, raw, grouped, codes, scales = op
+            lo, hi = a0 * width, a1 * width
+            nc.vector.quantize_mx(
+                out=codes[:, lo:hi].bitcast(FP8X4),
+                scales=scales[:, lo:hi],
+                in_=grouped[:, lo:hi, :].rearrange("p n j -> p (n j)"),
+            )
 
-        x_raw = {}
-        w_raw = {}
-        for a in range(PASSES):
-            x_raw[0, a] = load(x[rows(a), 0:HALF], f"x0_{a}")
-            w_raw[0, a] = load(w[rows(a), 0:P], f"w0_{a}")
-        nc.sync.dma_start(out=bias_rows[0 : M // P, :], in_=b.rearrange("(c p) -> c p", p=P))
-        nc.sync.dma_start(offsets[:], offs)
-        nc.sync.dma_start(out=weights[:], in_=wgo)
-        for a in range(PASSES):
-            x_raw[1, a] = load(x[rows(a), HALF:S], f"x1_{a}")
-        for i, (m0, count) in enumerate(BLOCKS):
-            if i > 0:
-                for a in range(PASSES):
-                    w_raw[i, a] = load(w[rows(a), m0 * P : (m0 + count) * P], f"w{i}_{a}")
-
-        for m in range(M // P):
-            nc.vector.memset(windows[m][:], 0.0)
-
-        make_identity(nc, ident[:])
-        bias_ps = bias_pool.tile([P, P], F32, name="bias_ps")
-        nc.tensor.transpose(bias_ps[:], bias_rows[:], ident[:])
-        nc.scalar.copy(out=bias[:], in_=bias_ps[:, 0 : M // P])
-
-        w_codes = {}
-        w_scales = {}
-
-        def w_cast(i, engines):
-            return [cast(engines[a], w_raw[i, a], f"w{i}_{a}") for a in range(PASSES)]
-
-        def w_quantize(i, a, grouped):
-            width = BLOCKS[i][1] * P
-            w_codes[i, a] = keep.tile([P, width], U32, align_bytes=64, name=f"w_codes{i}_{a}")
-            w_scales[i, a] = keep.tile([P, width], U8, align_bytes=64, name=f"w_scales{i}_{a}")
-            quantize(grouped, w_codes[i, a][:], w_scales[i, a][:])
-
-        def multiply(i, sub, s0, s1):
-            m = BLOCKS[i][0] + sub
-            cols = slice(sub * P, (sub + 1) * P)
-            acc = acc_pool.tile([P, S], F32, name="acc")
+        def product(acc_cols, wop, sub, xop):
+            wsrc, wwidth, wraw, wgrouped, wcodes, wscales = wop
+            xsrc, xwidth, xraw, xgrouped, xcodes, xscales = xop
             for a in range(PASSES):
+                w0 = a * wwidth + sub * P
+                x0 = a * xwidth
                 nc.tensor.matmul_mx(
-                    out=acc[:, s0:s1],
-                    lhsT=w_codes[i, a][:, cols].bitcast(FP8X4),
-                    lhsT_scale=w_scales[i, a][:, cols],
-                    rhs=x_codes[a][:, s0:s1].bitcast(FP8X4),
-                    rhs_scale=x_scales[a][:, s0:s1],
+                    out=acc_cols,
+                    lhsT=wcodes[:, w0 : w0 + P].bitcast(FP8X4),
+                    lhsT_scale=wscales[:, w0 : w0 + P],
+                    rhs=xcodes[:, x0 : x0 + xwidth].bitcast(FP8X4),
+                    rhs_scale=xscales[:, x0 : x0 + xwidth],
                     start=(a == 0),
                     stop=(a == PASSES - 1),
                 )
+
+        def gelu(m, acc, s0, s1):
             nc.scalar.activation(values[m][:, s0:s1], acc[:, s0:s1], GELU, bias=bias[:, m : m + 1])
 
         def scatter(m, h):
@@ -134,34 +105,76 @@ def tile_list_hscat_gelu_kernel(tc, x, w, b, wgo, offs, out):
                 MULT,
             )
 
-        def store(m):
-            nc.sync.dma_start(out=out[m * P : (m + 1) * P, :], in_=windows[m][:])
+        order = [(0, 0)]
+        for m in range(1, TILES):
+            order += [(m, 0), (m - 1, 1)]
+        order.append((TILES - 1, 1))
 
-        for a in range(PASSES):
-            gx = cast("V", x_raw[0, a], f"x0_{a}")
-            gw = cast("S", w_raw[0, a], f"w0_{a}")
-            quantize(gx, x_codes[a][:, 0:HALF], x_scales[a][:, 0:HALF])
-            w_quantize(0, a, gw)
-        multiply(0, 0, 0, HALF)
-        gx1 = [cast("SSV"[a], x_raw[1, a], f"x1_{a}") for a in range(PASSES)]
-        scatter(0, 0)
-        for a in range(PASSES):
-            quantize(gx1[a], x_codes[a][:, HALF:S], x_scales[a][:, HALF:S])
-        multiply(0, 0, HALF, S)
-        pending = [(0, 1)]
-        for i in range(1, len(BLOCKS)):
-            grouped = w_cast(i, "SSS")
-            for a in range(PASSES):
-                w_quantize(i, a, grouped[a])
-            m0, count = BLOCKS[i]
-            for sub in range(count):
-                multiply(i, sub, 0, S)
-            for m, h in pending:
+        def place(limit):
+            while order and order[0][0] < limit:
+                m, h = order.pop(0)
                 scatter(m, h)
                 if h == 1:
-                    store(m)
-            pending = [(m0 + sub, h) for h in range(2) for sub in range(count)]
-        for m, h in pending:
-            scatter(m, h)
-            if h == 1:
-                store(m)
+                    nc.sync.dma_start(out=out[m * P : (m + 1) * P, :], in_=windows[m][:])
+
+        xs = [operand(f"x{h}", x[:, h * HALF : (h + 1) * HALF]) for h in range(2)]
+        ws = [operand(f"w{i}", w[:, m0 * P : (m0 + count) * P]) for i, (m0, count) in enumerate(BLOCKS)]
+
+        for a in range(PASSES):
+            load(xs[0], a)
+            load(ws[0], a)
+        nc.sync.dma_start(out=bias_rows[0:TILES, :], in_=b.rearrange("(c p) -> c p", p=P))
+        nc.sync.dma_start(offsets[:], offs)
+        nc.sync.dma_start(out=weights[:], in_=wgo)
+        for op in [xs[1]] + ws[1:]:
+            for a in range(PASSES):
+                load(op, a)
+
+        make_identity(nc, ident[:])
+        for m in range(TILES):
+            (nc.vector if m < 4 else nc.gpsimd).memset(windows[m][:], 0.0)
+        bias_ps = bias_pool.tile([P, P], F32, name="bias_ps")
+        nc.tensor.transpose(bias_ps[:], bias_rows[:], ident[:])
+        nc.scalar.copy(out=bias[:], in_=bias_ps[:, 0:TILES])
+
+        def multiply(i):
+            m0, count = BLOCKS[i]
+            for sub in range(count):
+                acc = acc_pool.tile([P, S], F32, name="acc")
+                for h in range(2):
+                    product(acc[:, h * HALF : (h + 1) * HALF], ws[i], sub, xs[h])
+                gelu(m0 + sub, acc, 0, S)
+
+        def multiply_first(h):
+            acc = acc_pool.tile([P, S], F32, name="acc")
+            product(acc[:, 0:HALF], ws[0], 0, xs[h])
+            nc.scalar.activation(values[0][:, h * HALF : (h + 1) * HALF], acc[:, 0:HALF], GELU, bias=bias[:, 0:1])
+
+        casts = [[(0, 2, "S"), (2, 3, "S")]] * 6
+
+        def cast_all(i):
+            for a0, a1, engine in casts[i]:
+                cast(ws[i], a0, a1, engine)
+
+        for a in range(PASSES):
+            cast(xs[0], a, a + 1, "V")
+            cast(ws[0], a, a + 1, "S")
+            quantize(xs[0], a, a + 1)
+            quantize(ws[0], a, a + 1)
+        multiply_first(0)
+        for a0, a1, engine in [(0, 2, "S"), (2, 3, "S")]:
+            cast(xs[1], a0, a1, engine)
+        cast_all(1)
+        for a in range(PASSES):
+            quantize(xs[1], a, a + 1)
+        multiply_first(1)
+        place(1)
+        cast_all(2)
+        for i in range(1, len(BLOCKS)):
+            quantize(ws[i], 0, 2)
+            quantize(ws[i], 2, 3)
+            multiply(i)
+            if i + 2 < len(BLOCKS):
+                cast_all(i + 2)
+            place(BLOCKS[i][0])
+        place(TILES)

@@ -23,7 +23,7 @@ HALF = S // 2
 LIST_COLS = HALF // 16
 TILES = M // P
 
-BLOCKS = [(0, 1), (1, 1), (2, 2), (4, 2), (6, 1), (7, 1)]
+BLOCKS = [(m, 1) for m in range(TILES)]
 
 
 def tile_list_hscat_gelu_kernel(tc, x, w, b, wgo, offs, out):
@@ -40,7 +40,6 @@ def tile_list_hscat_gelu_kernel(tc, x, w, b, wgo, offs, out):
         ident = keep.tile([P, P], F32, name="ident")
         warm = keep.tile([P, 1], F32, name="warm")
         windows = [keep.tile([P, T], F32, name=f"window{m}") for m in range(TILES)]
-        values = [keep.tile([P, S], F32, name=f"values{m}") for m in range(TILES)]
 
         nc.vector.memset(warm[:], 0.0)
         nc.scalar.activation(warm[:], warm[:], GELU)
@@ -48,7 +47,7 @@ def tile_list_hscat_gelu_kernel(tc, x, w, b, wgo, offs, out):
 
         def operand(name, src):
             width = src.shape[1]
-            raw = keep.tile([P, PACK, PASSES, width], F32, name=f"{name}_raw")
+            raw = [keep.tile([P, PACK, width], F32, name=f"{name}_raw{a}") for a in range(PASSES)]
             grouped = keep.tile([P, PASSES * width, PACK], BF16, align_bytes=64, name=f"{name}_grouped")
             codes = keep.tile([P, PASSES * width], U32, align_bytes=64, name=f"{name}_codes")
             scales = keep.tile([P, PASSES * width], U8, align_bytes=64, name=f"{name}_scales")
@@ -57,16 +56,16 @@ def tile_list_hscat_gelu_kernel(tc, x, w, b, wgo, offs, out):
         def load(op, a, engine=nc.sync):
             src, width, raw, grouped, codes, scales = op
             rows = src[a * K_PASS : (a + 1) * K_PASS, :]
-            engine.dma_start(out=raw[:, :, a, :], in_=rows.rearrange("(p j) n -> p j n", j=PACK))
+            engine.dma_start(out=raw[a][:], in_=rows.rearrange("(p j) n -> p j n", j=PACK))
 
         def cast(op, a0, a1, engine, c0=0, c1=None):
             src, width, raw, grouped, codes, scales = op
             copy = nc.vector.tensor_copy if engine == "V" else nc.scalar.copy
-            lo, hi = a0 * width, a1 * width
-            copy(
-                out=grouped[:, lo:hi, :].rearrange("p (c i) t -> p c t i", i=4),
-                in_=raw[:].rearrange("p t a n -> p t (a n)")[:, :, lo:hi].rearrange("p t (c i) -> p c t i", i=4),
-            )
+            for a in range(a0, a1):
+                copy(
+                    out=grouped[:, a * width : (a + 1) * width, :].rearrange("p (c i) t -> p c t i", i=4),
+                    in_=raw[a][:].rearrange("p t (c i) -> p c t i", i=4),
+                )
 
         def quantize(op, a0, a1):
             src, width, raw, grouped, codes, scales = op
@@ -93,37 +92,43 @@ def tile_list_hscat_gelu_kernel(tc, x, w, b, wgo, offs, out):
                     stop=(a == PASSES - 1),
                 )
 
-        def gelu(m, acc, s0, s1):
-            nc.scalar.activation(values[m][:, s0:s1], acc[:, s0:s1], GELU, bias=bias[:, m : m + 1])
-
         def scatter(m, h):
             js = slice(h * HALF, (h + 1) * HALF)
             nc.vector.tensor_tensor(
                 windows[m][:].indirect(offsets[:, h * LIST_COLS : (h + 1) * LIST_COLS]),
-                values[m][:, js],
+                values[m, h],
                 weights[:, js],
                 MULT,
             )
 
-        order = [(0, 0)]
-        for m in range(1, TILES):
-            order += [(m, 0), (m - 1, 1)]
-        order.append((TILES - 1, 1))
-
-        def place(limit):
-            while order and order[0][0] < limit:
-                m, h = order.pop(0)
-                scatter(m, h)
-                if h == 1:
-                    nc.sync.dma_start(out=out[m * P : (m + 1) * P, :], in_=windows[m][:])
+        def store(m):
+            nc.sync.dma_start(out=out[m * P : (m + 1) * P, :], in_=windows[m][:])
 
         xs = [operand(f"x{h}", x[:, h * HALF : (h + 1) * HALF]) for h in range(2)]
-        ws = [operand(f"w{i}", w[:, m0 * P : (m0 + count) * P]) for i, (m0, count) in enumerate(BLOCKS)]
+        ws = [operand(f"w{m}", w[:, m * P : (m + 1) * P]) for m in range(TILES)]
+
+        def old_rows(m, a, h):
+            return ws[m][2][a][:].rearrange("p t n -> p (t n)")[:, h * HALF : (h + 1) * HALF]
+
+        spot = {(0, 0): (None, None), (0, 1): (1, 1), (TILES - 2, 0): (TILES - 1, 2), (TILES - 2, 1): (TILES - 1, 2)}
+        for m in range(1, TILES - 2):
+            for h in range(2):
+                spot[m, h] = (m + 2, 0)
+        values = {}
+        for m in range(TILES):
+            for h in range(2):
+                block, a = spot.get((m, h), (None, None))
+                if block is None:
+                    own = keep.tile([P, HALF], F32, name=f"values{m}_{h}")
+                    values[m, h] = own[:]
+                else:
+                    values[m, h] = old_rows(block, a, h)
 
         for a in range(PASSES):
             load(xs[0], a)
             load(ws[0], a)
-        nc.sync.dma_start(out=bias_rows[0:TILES, :], in_=b.rearrange("(c p) -> c p", p=P))
+            if a == 1:
+                nc.sync.dma_start(out=bias_rows[0:TILES, :], in_=b.rearrange("(c p) -> c p", p=P))
         nc.sync.dma_start(offsets[:], offs)
         nc.sync.dma_start(out=weights[:], in_=wgo)
         for op in [xs[1]] + ws[1:]:
@@ -133,48 +138,55 @@ def tile_list_hscat_gelu_kernel(tc, x, w, b, wgo, offs, out):
         make_identity(nc, ident[:])
         for m in range(TILES):
             (nc.vector if m < 4 else nc.gpsimd).memset(windows[m][:], 0.0)
-        bias_ps = bias_pool.tile([P, P], F32, name="bias_ps")
-        nc.tensor.transpose(bias_ps[:], bias_rows[:], ident[:])
-        nc.scalar.copy(out=bias[:], in_=bias_ps[:, 0:TILES])
 
-        def multiply(i):
-            m0, count = BLOCKS[i]
-            for sub in range(count):
+        def cast_block(m):
+            for a in range(PASSES):
+                cast(ws[m], a, a + 1, "V" if a == 2 and m in (1, 2, 3, 5) else "S")
+
+        accs = {}
+
+        def multiply(m, h):
+            if m == 0:
                 acc = acc_pool.tile([P, S], F32, name="acc")
-                for h in range(2):
-                    product(acc[:, h * HALF : (h + 1) * HALF], ws[i], sub, xs[h])
-                gelu(m0 + sub, acc, 0, S)
+                accs[m, h] = acc[:, 0:HALF]
+            elif h == 0:
+                acc = acc_pool.tile([P, S], F32, name="acc")
+                for g in range(2):
+                    accs[m, g] = acc[:, g * HALF : (g + 1) * HALF]
+            product(accs[m, h], ws[m], 0, xs[h])
 
-        def multiply_first(h):
-            acc = acc_pool.tile([P, S], F32, name="acc")
-            product(acc[:, 0:HALF], ws[0], 0, xs[h])
-            nc.scalar.activation(values[0][:, h * HALF : (h + 1) * HALF], acc[:, 0:HALF], GELU, bias=bias[:, 0:1])
-
-        casts = [[(0, 2, "S"), (2, 3, "S")]] * 6
-
-        def cast_all(i):
-            for a0, a1, engine in casts[i]:
-                cast(ws[i], a0, a1, engine)
+        def gelu(m, h):
+            nc.scalar.activation(values[m, h], accs[m, h], GELU, bias=bias[:, m : m + 1])
 
         for a in range(PASSES):
             cast(xs[0], a, a + 1, "V")
             cast(ws[0], a, a + 1, "S")
             quantize(xs[0], a, a + 1)
             quantize(ws[0], a, a + 1)
-        multiply_first(0)
-        for a0, a1, engine in [(0, 2, "S"), (2, 3, "S")]:
-            cast(xs[1], a0, a1, engine)
-        cast_all(1)
+        bias_ps = bias_pool.tile([P, P], F32, name="bias_ps")
+        nc.tensor.transpose(bias_ps[:], bias_rows[:], ident[:])
+        nc.scalar.copy(out=bias[:], in_=bias_ps[:, 0:TILES])
+        multiply(0, 0)
+        gelu(0, 0)
+        for a in range(PASSES):
+            cast(xs[1], a, a + 1, "V" if a == 2 else "S")
+        scatter(0, 0)
+        cast_block(1)
         for a in range(PASSES):
             quantize(xs[1], a, a + 1)
-        multiply_first(1)
-        place(1)
-        cast_all(2)
-        for i in range(1, len(BLOCKS)):
-            quantize(ws[i], 0, 2)
-            quantize(ws[i], 2, 3)
-            multiply(i)
-            if i + 2 < len(BLOCKS):
-                cast_all(i + 2)
-            place(BLOCKS[i][0])
-        place(TILES)
+        multiply(0, 1)
+        waiting = [(0, 1)]
+        for m in range(1, TILES):
+            if m + 1 < TILES:
+                cast_block(m + 1)
+            quantize(ws[m], 0, 2)
+            quantize(ws[m], 2, 3)
+            for h in range(2):
+                multiply(m, h)
+                waiting.append((m, h))
+            while waiting and (spot.get(waiting[0], (0, 0))[0] <= m + 1 or m == TILES - 1):
+                n, h = waiting.pop(0)
+                gelu(n, h)
+                scatter(n, h)
+                if h == 1:
+                    store(n)

@@ -110,10 +110,11 @@ def tile_list_hscat_gelu_kernel(tc, x, w, b, wgo, offs, out):
         def old_rows(m, a, h):
             return ws[m][2][a][:].rearrange("p t n -> p (t n)")[:, h * HALF : (h + 1) * HALF]
 
-        spot = {(0, 0): (None, None), (0, 1): (1, 1), (TILES - 2, 0): (TILES - 1, 2), (TILES - 2, 1): (TILES - 1, 2)}
-        for m in range(1, TILES - 2):
-            for h in range(2):
-                spot[m, h] = (m + 2, 0)
+        spot = {(0, 1): (1, 1), (1, 1): (2, 2), (TILES - 2, 1): (TILES - 1, 2)}
+        for m in range(1, TILES - 1):
+            spot[m, 0] = (m + 1, 1)
+            if 1 < m < TILES - 2:
+                spot[m, 1] = (m + 2, 2)
         values = {}
         for m in range(TILES):
             for h in range(2):
@@ -141,7 +142,7 @@ def tile_list_hscat_gelu_kernel(tc, x, w, b, wgo, offs, out):
 
         def cast_block(m):
             for a in range(PASSES):
-                cast(ws[m], a, a + 1, "V" if a == 2 and m in (1, 2, 3, 5) else "S")
+                cast(ws[m], a, a + 1, "V" if (m, a) == (1, 1) else "S")
 
         accs = {}
 
@@ -169,13 +170,14 @@ def tile_list_hscat_gelu_kernel(tc, x, w, b, wgo, offs, out):
         multiply(0, 0)
         gelu(0, 0)
         for a in range(PASSES):
-            cast(xs[1], a, a + 1, "V" if a == 2 else "S")
+            cast(xs[1], a, a + 1, "V" if a == 0 else "S")
         scatter(0, 0)
         cast_block(1)
         for a in range(PASSES):
             quantize(xs[1], a, a + 1)
         multiply(0, 1)
         waiting = [(0, 1)]
+        placed = [(0, 0)]
         for m in range(1, TILES):
             if m + 1 < TILES:
                 cast_block(m + 1)
@@ -184,9 +186,14 @@ def tile_list_hscat_gelu_kernel(tc, x, w, b, wgo, offs, out):
             for h in range(2):
                 multiply(m, h)
                 waiting.append((m, h))
-            while waiting and (spot.get(waiting[0], (0, 0))[0] <= m + 1 or m == TILES - 1):
-                n, h = waiting.pop(0)
+            still = []
+            for n, h in waiting:
+                if spot.get((n, h), (n, 0))[0] > m + 1 or (n == m and m < TILES - 1 and (n, h) not in spot):
+                    still.append((n, h))
+                    continue
                 gelu(n, h)
                 scatter(n, h)
-                if h == 1:
+                placed.append((n, h))
+                if (n, 1 - h) in placed:
                     store(n)
+            waiting = still

from contextlib import ExitStack

import concourse.mybir as mybir
from concourse.masks import make_identity

K, M, T, S = 1536, 1024, 512, 256
FLOPS = 2 * K * M * S

F32 = mybir.dt.float32
BF16 = mybir.dt.bfloat16
U32 = mybir.dt.uint32
U16 = mybir.dt.uint16
U8 = mybir.dt.uint8
FP8X4 = mybir.dt.float8_e4m3fn_x4
GELU = mybir.ActivationFunctionType.Gelu_apprx_tanh
MULT = mybir.AluOpType.mult

P = 128
PACK = 4
K_PASS = P * PACK
PASSES = K // K_PASS
HALF = S // 2
LIST_COLS = HALF // 16
TILES = M // P

BLOCKS = [(m, 1) for m in range(TILES)]


def tile_list_hscat_gelu_kernel(tc, x, w, b, wgo, offs, out):
    nc = tc.nc
    with ExitStack() as ctx:
        keep = ctx.enter_context(tc.tile_pool(name="keep", bufs=1))
        acc_pool = ctx.enter_context(tc.psum_pool(name="acc", bufs=7))
        bias_pool = ctx.enter_context(tc.psum_pool(name="bias", bufs=1))

        offsets = keep.tile([P, S // 16], U16, name="offsets")
        weights = keep.tile([P, S], F32, name="weights")
        bias_rows = keep.tile([P, P], F32, name="bias_rows")
        bias = keep.tile([P, TILES], F32, name="bias_cols")
        ident = keep.tile([P, P], F32, name="ident")
        warm = keep.tile([P, 1], F32, name="warm")
        windows = [keep.tile([P, T], F32, name=f"window{m}") for m in range(TILES)]

        nc.vector.memset(warm[:], 0.0)
        nc.scalar.activation(warm[:], warm[:], GELU)
        nc.gpsimd.memset(bias_rows[:], 0.0)

        def operand(name, src):
            width = src.shape[1]
            raw = [keep.tile([P, PACK, width], F32, name=f"{name}_raw{a}") for a in range(PASSES)]
            grouped = keep.tile([P, PASSES * width, PACK], BF16, align_bytes=64, name=f"{name}_grouped")
            codes = keep.tile([P, PASSES * width], U32, align_bytes=64, name=f"{name}_codes")
            scales = keep.tile([P, PASSES * width], U8, align_bytes=64, name=f"{name}_scales")
            return src, width, raw, grouped, codes, scales

        def load(op, a, engine=nc.sync):
            src, width, raw, grouped, codes, scales = op
            rows = src[a * K_PASS : (a + 1) * K_PASS, :]
            engine.dma_start(out=raw[a][:], in_=rows.rearrange("(p j) n -> p j n", j=PACK))

        def cast(op, a0, a1, engine, c0=0, c1=None):
            src, width, raw, grouped, codes, scales = op
            copy = nc.vector.tensor_copy if engine == "V" else nc.scalar.copy
            for a in range(a0, a1):
                copy(
                    out=grouped[:, a * width : (a + 1) * width, :].rearrange("p (c i) t -> p c t i", i=4),
                    in_=raw[a][:].rearrange("p t (c i) -> p c t i", i=4),
                )

        def quantize(op, a0, a1):
            src, width, raw, grouped, codes, scales = op
            lo, hi = a0 * width, a1 * width
            nc.vector.quantize_mx(
                out=codes[:, lo:hi].bitcast(FP8X4),
                scales=scales[:, lo:hi],
                in_=grouped[:, lo:hi, :].rearrange("p n j -> p (n j)"),
            )

        def product(acc_cols, wop, sub, xop):
            wsrc, wwidth, wraw, wgrouped, wcodes, wscales = wop
            xsrc, xwidth, xraw, xgrouped, xcodes, xscales = xop
            for a in range(PASSES):
                w0 = a * wwidth + sub * P
                x0 = a * xwidth
                nc.tensor.matmul_mx(
                    out=acc_cols,
                    lhsT=wcodes[:, w0 : w0 + P].bitcast(FP8X4),
                    lhsT_scale=wscales[:, w0 : w0 + P],
                    rhs=xcodes[:, x0 : x0 + xwidth].bitcast(FP8X4),
                    rhs_scale=xscales[:, x0 : x0 + xwidth],
                    start=(a == 0),
                    stop=(a == PASSES - 1),
                )

        def scatter(m, h):
            js = slice(h * HALF, (h + 1) * HALF)
            nc.vector.tensor_tensor(
                windows[m][:].indirect(offsets[:, h * LIST_COLS : (h + 1) * LIST_COLS]),
                values[m, h],
                weights[:, js],
                MULT,
            )

        def store(m):
            nc.sync.dma_start(out=out[m * P : (m + 1) * P, :], in_=windows[m][:])

        xs = [operand(f"x{h}", x[:, h * HALF : (h + 1) * HALF]) for h in range(2)]
        ws = [operand(f"w{m}", w[:, m * P : (m + 1) * P]) for m in range(TILES)]

        def old_rows(m, a, h):
            return ws[m][2][a][:].rearrange("p t n -> p (t n)")[:, h * HALF : (h + 1) * HALF]

        spot = {(0, 1): (1, 1), (1, 1): (2, 2), (TILES - 2, 1): (TILES - 1, 2)}
        for m in range(1, TILES - 1):
            spot[m, 0] = (m + 1, 1)
            if 1 < m < TILES - 2:
                spot[m, 1] = (m + 2, 2)
        values = {}
        for m in range(TILES):
            for h in range(2):
                block, a = spot.get((m, h), (None, None))
                if block is None:
                    own = keep.tile([P, HALF], F32, name=f"values{m}_{h}")
                    values[m, h] = own[:]
                else:
                    values[m, h] = old_rows(block, a, h)

        for a in range(PASSES):
            load(xs[0], a)
            load(ws[0], a)
            if a == 1:
                nc.sync.dma_start(out=bias_rows[0:TILES, :], in_=b.rearrange("(c p) -> c p", p=P))
        nc.sync.dma_start(offsets[:], offs)
        nc.sync.dma_start(out=weights[:], in_=wgo)
        for op in [xs[1]] + ws[1:]:
            for a in range(PASSES):
                load(op, a)

        make_identity(nc, ident[:])
        for m in range(TILES):
            (nc.vector if m < 4 else nc.gpsimd).memset(windows[m][:], 0.0)

        def cast_block(m):
            for a in range(PASSES):
                cast(ws[m], a, a + 1, "V" if (m, a) == (1, 1) else "S")

        accs = {}

        def multiply(m, h):
            if m == 0:
                acc = acc_pool.tile([P, S], F32, name="acc")
                accs[m, h] = acc[:, 0:HALF]
            elif h == 0:
                acc = acc_pool.tile([P, S], F32, name="acc")
                for g in range(2):
                    accs[m, g] = acc[:, g * HALF : (g + 1) * HALF]
            product(accs[m, h], ws[m], 0, xs[h])

        def gelu(m, h):
            nc.scalar.activation(values[m, h], accs[m, h], GELU, bias=bias[:, m : m + 1])

        for a in range(PASSES):
            cast(xs[0], a, a + 1, "V")
            cast(ws[0], a, a + 1, "S")
            quantize(xs[0], a, a + 1)
            quantize(ws[0], a, a + 1)
        bias_ps = bias_pool.tile([P, P], F32, name="bias_ps")
        nc.tensor.transpose(bias_ps[:], bias_rows[:], ident[:])
        nc.scalar.copy(out=bias[:], in_=bias_ps[:, 0:TILES])
        multiply(0, 0)
        gelu(0, 0)
        for a in range(PASSES):
            cast(xs[1], a, a + 1, "V" if a == 0 else "S")
        scatter(0, 0)
        cast_block(1)
        for a in range(PASSES):
            quantize(xs[1], a, a + 1)
        multiply(0, 1)
        waiting = [(0, 1)]
        placed = [(0, 0)]
        for m in range(1, TILES):
            if m + 1 < TILES:
                cast_block(m + 1)
            quantize(ws[m], 0, 2)
            quantize(ws[m], 2, 3)
            for h in range(2):
                multiply(m, h)
                waiting.append((m, h))
            still = []
            for n, h in waiting:
                if spot.get((n, h), (n, 0))[0] > m + 1 or (n == m and m < TILES - 1 and (n, h) not in spot):
                    still.append((n, h))
                    continue
                gelu(n, h)
                scatter(n, h)
                placed.append((n, h))
                if (n, 1 - h) in placed:
                    store(n)
            waiting = still
